import numpy as np
import ml_dtypes


def mxq(x, axis, fmt="e4m3"):
    dtype, down = {"e4m3": (ml_dtypes.float8_e4m3fn, 7), "e5m2": (ml_dtypes.float8_e5m2, 14)}[fmt]
    v = np.moveaxis(np.asarray(x, np.float32).astype(ml_dtypes.bfloat16).astype(np.float64), axis, -1)
    blocks = v.reshape(v.shape[:-1] + (-1, 32))
    amax = np.abs(blocks).max(-1, keepdims=True)
    byte = np.maximum(np.where(amax > 0, np.frexp(amax)[1] - 1 + 127, 0) - down, 1)
    scale = np.exp2(byte - 127.0)
    codes = (blocks / scale).astype(np.float32).astype(dtype).astype(np.float64)
    return np.moveaxis((codes * scale).reshape(v.shape), -1, axis)


WIDE = False


def mx_kscale(k):
    if not WIDE:
        return np.ones(k)
    levels = np.array([10, -10, 5, -5, 0])
    if k % 512:
        return np.exp2(np.random.permutation(np.resize(levels, k // 32))).repeat(32)
    a = np.empty((k // 512, 16))
    for p in range(k // 512):
        a[p, :8] = np.random.permutation(np.resize(levels, 8))
        for g in range(8):
            far = levels[np.abs(levels - a[p, g]) >= 10]
            a[p, g + 8] = far[np.random.randint(len(far))]
    return np.exp2(a.ravel()).repeat(32)


def f64(x):
    return np.asarray(x).astype(np.float64)


def striped(idx):
    return np.tile(idx.reshape(-1, 16).T, (8, 1)).astype(np.uint16)


def unstriped(offs):
    return offs[:16].T.reshape(-1).astype(np.int64)


def d_silu(v):
    s = 1.0 / (1.0 + np.exp(-np.maximum(v, -700.0)))
    return s * (1.0 + v * (1.0 - s))


K, T, E, C, H, N = 128, 512, 8, 128, 1024, 1024


def by_expert(wq, xq):
    return np.concatenate([wq[e].T @ xq[:, e * C:(e + 1) * C] for e in range(E)], axis=1)


def setup_inputs():
    n = np.random.standard_normal
    s = mx_kscale(N)[:, None]
    u = mx_kscale(H)
    first = np.random.permutation(np.repeat(np.arange(E), T // E))
    second = (first + 1 + np.random.permutation(np.repeat(np.arange(E - 1), -(-T // (E - 1)))[:T])) % E
    while np.bincount(second, minlength=E).max() != T // E:
        load = np.bincount(second, minlength=E); hi, lo = int(load.argmax()), int(load.argmin())
        t = np.flatnonzero((second == hi) & (first != lo))[0]; second[t] = lo
    slot_token = np.empty(E * C, np.int64); pos = np.empty((2, T), np.int64); fill = np.zeros(E, np.int64)
    place = np.stack([np.random.permutation(C) for _ in range(E)])
    for r, deal in enumerate((first, second)):
        for t in np.random.permutation(T):
            e = deal[t]; j = e * C + place[e, fill[e]]; fill[e] += 1; slot_token[j] = t; pos[r, t] = j
    g = np.random.uniform(0.2, 0.8, T)
    w_slot = np.empty(E * C); w_slot[pos[0]] = g; w_slot[pos[1]] = 1.0 - g
    return {
        "dyT": (n((N, T)) * s).astype(np.float32),
        "a": n((H, E * C)).astype(np.float32),
        "w2": (n((E, N, H)) / np.sqrt(N) / s[None] * u[None, None, :]).astype(np.float32),
        "w1": (n((E, H, K)) / np.sqrt(H) / u[None, :, None]).astype(np.float32),
        "gate": np.tile(w_slot, (N, 1)).astype(np.float32),
        "offs": striped(slot_token),
        "pos1": striped(pos[0]),
        "pos2": striped(pos[1]),
    }


def reference(dyT, a, w2, w1, gate, offs, pos1, pos2):
    idx = unstriped(offs)
    gq = mxq(f64(gate) * f64(dyT)[:, idx], 0, "e4m3")
    dh = by_expert(mxq(f64(w2), 1, "e4m3"), gq)
    da = dh * d_silu(f64(a))
    dx = by_expert(mxq(f64(w1), 1, "e4m3"), mxq(da, 0, "e4m3"))
    return dx[:, unstriped(pos1)] + dx[:, unstriped(pos2)]

@@ -1,0 +1,308 @@
+from contextlib import ExitStack
+
+import concourse.mybir as mybir
+
+F32 = mybir.dt.float32
+BF16 = mybir.dt.bfloat16
+U32 = mybir.dt.uint32
+U16 = mybir.dt.uint16
+U8 = mybir.dt.uint8
+FP8X4 = mybir.dt.float8_e4m3fn_x4
+
+MULT = mybir.AluOpType.mult
+ADD = mybir.AluOpType.add
+SUB = mybir.AluOpType.subtract
+SIGMOID = mybir.ActivationFunctionType.Sigmoid
+
+P = 128
+E, C, T = 8, 128, 512
+N, H, K = 1024, 1024, 128
+S = E * C
+Q = 4
+HALF = S // 2
+PAD = 8
+
+FLOPS = 2 * S * H * (N + K)
+BYTES = 4 * (N * T + H * S + E * N * H + E * H * K + S + K * T) + 2 * (128 * 64 + 2 * 128 * 32)
+
+VECTOR_PIECES = {(0, 0, 1), (0, 1, 0), (1, 1, 0), (2, 0, 1), (3, 0, 0), (3, 0, 1), (3, 1, 1), (4, 1, 1), (5, 1, 0), (6, 0, 1), (7, 0, 0), (7, 1, 1)}
+BACKGROUND = [(0, "I00"), (0, "G100"), (0, "G101"), (0, "G102"), (0, "G103"), (0, "S000"), (0, "I10"), (0, "Q00"), (1, "S010"), (1, "T000"), (2, "Z000"), (2, "T010"), (3, "Q10"), (3, "W0"), (3, "S001"), (3, "G010"), (4, "S011"), (4, "Z010"), (4, "G012"), (4, "G013"), (5, "G110"), (6, "G011"), (7, "T001"), (7, "I01"), (8, "R0"), (8, "T011"), (8, "G111"), (8, "G112"), (9, "W1"), (9, "G113"), (11, "S110"), (11, "R1"), (11, "S100"), (11, "Z001"), (11, "Z011"), (13, "I11"), (13, "S111"), (13, "T110"), (14, "S101"), (15, "T100"), (17, "Q01"), (17, "T101"), (18, "W2"), (19, "Q11"), (19, "T111"), (19, "Z100"), (20, "Z110"), (21, "Z101"), (21, "Z111"), (24, "R2"), (31, "W3"), (34, "R3")]
+LAGS = [(10, "mm2"), (5, "mm1"), (5, "da0"), (10, "dxc"), (8, "qda"), (5, "da1")]
+
+
+def tile_moe_bdx_mlp_silu_kernel(tc, dyT, a, w2, w1, gate, offs, pos1, pos2, out):
+    nc = tc.nc
+    with ExitStack() as ctx:
+        pool = ctx.enter_context(tc.tile_pool(name="sb", bufs=1))
+        psum = ctx.enter_context(tc.psum_pool(name="ps", bufs=1))
+
+        warm = pool.tile([P, 8], F32, name="warm")
+        nc.gpsimd.memset(warm[:], 0.0)
+        nc.scalar.activation(warm[:], warm[:], SIGMOID)
+
+        offs_sb = pool.tile([P, S // 16], U16, name="offs_sb")
+        pos1_sb = pool.tile([P, T // 16], U16, name="pos1_sb")
+        pos2_sb = pool.tile([P, T // 16], U16, name="pos2_sb")
+        gate_sb = pool.tile([P, S], F32, name="gate_sb")
+        dx_sb = pool.tile([P, S], F32, name="dx_sb")
+
+        dy = {}
+        for c in range(2):
+            for t in range(Q):
+                d = pool.tile([P, T + PAD], F32, name="dy", tag="dy", bufs=8)
+                nc.gpsimd.memset(d[:, T:], 0.0)
+                dy[c, t] = d
+
+        def load_lists():
+            nc.sync.dma_start(out=offs_sb[:], in_=offs)
+
+        def load_pos():
+            nc.sync.dma_start(out=pos1_sb[:], in_=pos1)
+            nc.sync.dma_start(out=pos2_sb[:], in_=pos2)
+
+        def load_dy(c, t):
+            rows = dyT[512 * c : 512 * (c + 1), :].rearrange("(p t) j -> t p j", t=Q)
+            nc.sync.dma_start(out=dy[c, t][:, 0:T], in_=rows[t, :, :])
+
+        def load_gate(half):
+            cols = slice(HALF * half, HALF * (half + 1))
+            nc.sync.dma_start(out=gate_sb[:, cols], in_=gate[0:P, cols])
+
+        raw = {}
+
+        def load_w2(e, c, h=None):
+            rows = w2[e, 512 * c : 512 * (c + 1), :].rearrange("(p j) i -> p j i", j=Q)
+            if h is None:
+                r = pool.tile([P, Q, H], F32, name="raw", tag="raw", bufs=4)
+                nc.sync.dma_start(out=r[:], in_=rows)
+                raw[e, c, 0] = r[:, :, 0:512]
+                raw[e, c, 1] = r[:, :, 512:1024]
+            else:
+                r = pool.tile([P, Q, 512], F32, name="raw", tag="raw", bufs=4)
+                nc.sync.dma_start(out=r[:], in_=rows[:, :, 512 * h : 512 * (h + 1)])
+                raw[e, c, h] = r[:]
+
+        av = {}
+
+        def load_a(half, h):
+            v = pool.tile([P, Q, HALF], F32, name="av", tag="av", bufs=2)
+            cols = slice(HALF * half, HALF * (half + 1))
+            nc.sync.dma_start(out=v[:], in_=a[512 * h : 512 * (h + 1), cols].rearrange("(p t) j -> p t j", t=Q))
+            av[half, h] = v
+
+        w1raw = {}
+
+        def load_w1(pair):
+            r = pool.tile([P, 4, Q, K], F32, name="w1raw", tag="w1raw", bufs=1)
+            rows = w1[2 * pair : 2 * pair + 2, :, :].rearrange("e (h p j) k -> p (e h) j k", h=2, j=Q)
+            nc.sync.dma_start(out=r[:], in_=rows)
+            w1raw[pair] = r
+
+        gf, gb, gcodes, gscales = {}, {}, {}, {}
+
+        def gather(c, half, t):
+            if t == 0:
+                f = pool.tile([P, Q, HALF], F32, name="gf", tag="gf", bufs=2)
+                gf[c, half] = f
+            cols = slice(HALF * half, HALF * (half + 1))
+            lst = slice(32 * half, 32 * (half + 1))
+            nc.vector.tensor_tensor(
+                gf[c, half][:, t, :], dy[c, t][:].indirect(offs_sb[:, lst]), gate_sb[:, cols], MULT
+            )
+
+        def gint(c, half):
+            b = pool.tile([P, HALF, Q], BF16, name="gb", tag="gb", bufs=2, align_bytes=64)
+            nc.scalar.copy(
+                out=b[:].rearrange("p (c i) t -> p c t i", i=4),
+                in_=gf[c, half][:].rearrange("p t (c i) -> p c t i", i=4),
+            )
+            gb[c, half] = b
+
+        def qg(c, half):
+            codes = pool.tile([P, HALF], U32, name="gcodes", tag="gcodes", bufs=4, align_bytes=64)
+            scales = pool.tile([P, HALF], U8, name="gscales", tag="gscales", bufs=4, align_bytes=64)
+            nc.vector.quantize_mx(
+                out=codes[:].bitcast(FP8X4), scales=scales[:], in_=gb[c, half][:].rearrange("p s t -> p (s t)")
+            )
+            gcodes[c, half], gscales[c, half] = codes, scales
+
+        dneg = {}
+
+        def sig(half, h, pair):
+            z = pool.tile([P, Q, 256], F32, name="dneg", tag="dneg", bufs=6)
+            nc.scalar.activation(z[:], av[half, h][:, :, 256 * pair : 256 * (pair + 1)], SIGMOID)
+            dneg[half, h, pair] = z
+
+        def t1(half, h, pair):
+            z, v = dneg[half, h, pair], av[half, h][:, :, 256 * pair : 256 * (pair + 1)]
+            nc.vector.scalar_tensor_tensor(out=v, in0=z[:], scalar=1.0, in1=v, op0=SUB, op1=MULT)
+
+        def zz(half, h, pair):
+            z, v = dneg[half, h, pair], av[half, h][:, :, 256 * pair : 256 * (pair + 1)]
+            nc.vector.scalar_tensor_tensor(out=z[:], in0=v, scalar=1.0, in1=z[:], op0=SUB, op1=MULT)
+
+        wb, wcodes, wscales = {}, {}, {}
+
+        def inter(e, c, h):
+            b = pool.tile([P, 512 * Q], BF16, name="wb", tag="wb", bufs=5, align_bytes=64)
+            dst = b[:].rearrange("p (t m j) -> p m j t", t=4, j=Q)
+            src = raw[e, c, h].rearrange("p j (m t) -> p m j t", t=4)
+            if (e, c, h) in VECTOR_PIECES:
+                nc.vector.tensor_copy(out=dst, in_=src)
+            else:
+                nc.scalar.copy(out=dst, in_=src)
+            wb[e, c, h] = b
+
+        def qw(e, c, h):
+            codes = pool.tile([P, 512], U32, name="wcodes", tag="wcodes", bufs=8, align_bytes=64)
+            scales = pool.tile([P, 512], U8, name="wscales", tag="wscales", bufs=8, align_bytes=64)
+            nc.vector.quantize_mx(out=codes[:].bitcast(FP8X4), scales=scales[:], in_=wb[e, c, h][:])
+            wcodes[e, c, h], wscales[e, c, h] = codes, scales
+
+        w1b, w1codes, w1scales = {}, {}, {}
+
+        def w1i(pair):
+            b = pool.tile([P, 4, K, Q], BF16, name="w1b", tag="w1b", bufs=1, align_bytes=64)
+            nc.scalar.copy(out=b[:], in_=w1raw[pair][:].rearrange("p x j k -> p x k j"))
+            w1b[pair] = b
+
+        def w1q(pair):
+            codes = pool.tile([P, 4, K], U32, name="w1codes", tag="w1codes", bufs=2, align_bytes=64)
+            scales = pool.tile([P, 4, K], U8, name="w1scales", tag="w1scales", bufs=2, align_bytes=64)
+            nc.vector.quantize_mx(
+                out=codes[:].rearrange("p x k -> p (x k)").bitcast(FP8X4),
+                scales=scales[:].rearrange("p x k -> p (x k)"),
+                in_=w1b[pair][:].rearrange("p x k j -> p (x k j)"),
+            )
+            w1codes[pair], w1scales[pair] = codes, scales
+
+        dh = {}
+
+        def mm1(e):
+            half = e // 4
+            slots = slice(C * (e % 4), C * (e % 4 + 1))
+            for h in range(2):
+                acc = psum.tile([P, Q, C], F32, name="dh", tag="dh", bufs=6)
+                for t in range(Q):
+                    cols = slice(P * t, P * (t + 1))
+                    for c in range(2):
+                        nc.tensor.matmul_mx(
+                            out=acc[:, t, :],
+                            lhsT=wcodes[e, c, h][:, cols].bitcast(FP8X4),
+                            lhsT_scale=wscales[e, c, h][:, cols],
+                            rhs=gcodes[c, half][:, slots].bitcast(FP8X4),
+                            rhs_scale=gscales[c, half][:, slots],
+                            start=(c == 0),
+                            stop=(c == 1),
+                        )
+                dh[e, h] = acc
+
+        dab, dacodes, dascales = {}, {}, {}
+
+        def da(e, h):
+            if h == 0:
+                b = pool.tile([P, 2, C, Q], BF16, name="dab", tag="dab", bufs=2, align_bytes=64)
+                dab[e] = b
+            slots = slice(C * (e % 2), C * (e % 2 + 1))
+            nc.vector.scalar_tensor_tensor(
+                out=dab[e][:, h],
+                in0=dh[e, h][:].rearrange("p t j -> p j t"),
+                scalar=-1.0,
+                in1=dneg[e // 4, h, (e % 4) // 2][:, :, slots].rearrange("p t j -> p j t"),
+                op0=MULT,
+                op1=MULT,
+            )
+
+        def qda(e):
+            codes = pool.tile([P, 2, C], U32, name="dacodes", tag="dacodes", bufs=2, align_bytes=64)
+            scales = pool.tile([P, 2, C], U8, name="dascales", tag="dascales", bufs=2, align_bytes=64)
+            nc.vector.quantize_mx(
+                out=codes[:].rearrange("p h j -> p (h j)").bitcast(FP8X4),
+                scales=scales[:].rearrange("p h j -> p (h j)"),
+                in_=dab[e][:].rearrange("p h j t -> p (h j t)"),
+            )
+            dacodes[e], dascales[e] = codes, scales
+
+        dxp = {}
+
+        def mm2(e):
+            acc = psum.tile([P, C], F32, name="dx", tag="dx", bufs=2)
+            for h in range(2):
+                x = 2 * (e % 2) + h
+                nc.tensor.matmul_mx(
+                    out=acc[:],
+                    lhsT=w1codes[e // 2][:, x, :].bitcast(FP8X4),
+                    lhsT_scale=w1scales[e // 2][:, x, :],
+                    rhs=dacodes[e][:, h, :].bitcast(FP8X4),
+                    rhs_scale=dascales[e][:, h, :],
+                    start=(h == 0),
+                    stop=(h == 1),
+                )
+            dxp[e] = acc
+
+        def dxc(e):
+            nc.scalar.copy(out=dx_sb[:, C * e : C * (e + 1)], in_=dxp[e][:])
+
+        load_lists()
+        load_gate(0)
+        for t in range(Q):
+            load_dy(0, t)
+            if t == 3:
+                load_w2(0, 0, 0)
+        load_dy(1, 0)
+        load_dy(1, 1)
+        load_w2(0, 0, 1)
+        load_dy(1, 2)
+        load_dy(1, 3)
+        load_a(0, 0)
+        load_w2(0, 1, 0)
+        load_a(0, 1)
+        load_w2(0, 1, 1)
+        load_w1(0)
+        load_gate(1)
+        load_pos()
+        for e in range(1, E):
+            if e < E - 1:
+                load_w2(e, 0)
+                load_w2(e, 1)
+            else:
+                load_w1(3)
+                for h in range(2):
+                    for c in range(2):
+                        load_w2(e, c, h)
+            if e in (2, 4):
+                load_w1(e // 2)
+            if e == 2:
+                load_a(1, 0)
+                load_a(1, 1)
+
+        def background(item):
+            op, args = item[0], [int(x) for x in item[1:]]
+            {"G": gather, "I": gint, "Q": qg, "S": sig, "T": t1, "Z": zz, "W": w1i, "R": w1q}[op](*args)
+
+        for t in range(Q):
+            gather(0, 0, t)
+        pieces = [(e, c, h) for e in range(E - 1) for c in range(2) for h in range(2)]
+        pieces += [(E - 1, c, h) for h in range(2) for c in range(2)]
+        stages = {"mm1": mm1, "da0": lambda e: da(e, 0), "da1": lambda e: da(e, 1), "qda": qda, "mm2": mm2, "dxc": dxc}
+        for g in range(4 * E + 10):
+            if g < 4 * E:
+                inter(*pieces[g])
+            for at, item in BACKGROUND:
+                if at == g:
+                    background(item)
+            if 1 <= g <= 4 * E:
+                qw(*pieces[g - 1])
+            for lag, stage in LAGS:
+                if g >= lag and (g - lag) % 4 == 0 and (g - lag) // 4 < E:
+                    stages[stage]((g - lag) // 4)
+
+        for s in range(2):
+            lst = slice(16 * s, 16 * (s + 1))
+            g1 = pool.tile([P, T // 2], F32, name="g1", tag="g1", bufs=2)
+            g2 = pool.tile([P, T // 2], F32, name="g2", tag="g2", bufs=2)
+            res = pool.tile([P, T // 2], F32, name="res", tag="res", bufs=2)
+            nc.vector.tensor_copy(g1[:], dx_sb[:].indirect(pos1_sb[:, lst]))
+            nc.vector.tensor_copy(g2[:], dx_sb[:].indirect(pos2_sb[:, lst]))
+            nc.vector.tensor_tensor(res[:], g1[:], g2[:], ADD)
+            nc.sync.dma_start(out=out[:, 256 * s : 256 * (s + 1)], in_=res[:])

@@ -25,9 +25,10 @@ PAD = 8
 FLOPS = 2 * S * H * (N + K)
 BYTES = 4 * (N * T + H * S + E * N * H + E * H * K + S + K * T) + 2 * (128 * 64 + 2 * 128 * 32)
 
-VECTOR_PIECES = {(0, 0, 1), (0, 1, 0), (1, 1, 0), (2, 0, 1), (3, 0, 0), (3, 0, 1), (3, 1, 1), (4, 1, 1), (5, 1, 0), (6, 0, 1), (7, 0, 0), (7, 1, 1)}
-BACKGROUND = [(0, "I00"), (0, "G100"), (0, "G101"), (0, "G102"), (0, "G103"), (0, "S000"), (0, "I10"), (0, "Q00"), (1, "S010"), (1, "T000"), (2, "Z000"), (2, "T010"), (3, "Q10"), (3, "W0"), (3, "S001"), (3, "G010"), (4, "S011"), (4, "Z010"), (4, "G012"), (4, "G013"), (5, "G110"), (6, "G011"), (7, "T001"), (7, "I01"), (8, "R0"), (8, "T011"), (8, "G111"), (8, "G112"), (9, "W1"), (9, "G113"), (11, "S110"), (11, "R1"), (11, "S100"), (11, "Z001"), (11, "Z011"), (13, "I11"), (13, "S111"), (13, "T110"), (14, "S101"), (15, "T100"), (17, "Q01"), (17, "T101"), (18, "W2"), (19, "Q11"), (19, "T111"), (19, "Z100"), (20, "Z110"), (21, "Z101"), (21, "Z111"), (24, "R2"), (31, "W3"), (34, "R3")]
-LAGS = [(10, "mm2"), (5, "mm1"), (5, "da0"), (10, "dxc"), (8, "qda"), (5, "da1")]
+VECTOR_PIECES = {(7, 1, 0), (7, 0, 0), (2, 0, 1), (4, 0, 0), (4, 1, 1), (2, 0, 0), (0, 1, 0), (5, 1, 0), (2, 1, 0)}
+BACKGROUND = [(0, "G100"), (0, "G102"), (2, "G103"), (2, "G010"), (2, "I00"), (3, "G013"), (4, "Q00"), (4, "G011"), (5, "G101"), (6, "W0"), (6, "I10"), (8, "G110"), (9, "Q10"), (11, "G111"), (12, "G112"), (12, "W1"), (12, "G012"), (12, "R0"), (13, "I01"), (14, "G113"), (17, "Q01"), (18, "I11"), (18, "W2"), (19, "R1"), (20, "Q11"), (20, "R2"), (25, "W3"), (34, "R3")]
+LAST = [(9, "qda"), (13, "mm2"), (5, "mm11"), (1, "sig"), (1, "t1"), (7, "da0"), (3, "mm10"), (7, "da1"), (13, "dxc"), (3, "z")]
+LAGS = [(10, "da0"), (13, "mm2"), (13, "dxc"), (1, "sig"), (10, "mm11"), (9, "mm10"), (3, "t1"), (4, "z"), (12, "qda"), (10, "da1")]
 
 
 def tile_moe_bdx_mlp_silu_kernel(tc, dyT, a, w2, w1, gate, offs, pos1, pos2, out):
@@ -85,7 +86,7 @@ def tile_moe_bdx_mlp_silu_kernel(tc, dyT, a, w2, w1, gate, offs, pos1, pos2, out
         av = {}
 
         def load_a(half, h):
-            v = pool.tile([P, Q, HALF], F32, name="av", tag="av", bufs=2)
+            v = pool.tile([P, Q, HALF], F32, name="av", tag="av", bufs=4)
             cols = slice(HALF * half, HALF * (half + 1))
             nc.sync.dma_start(out=v[:], in_=a[512 * h : 512 * (h + 1), cols].rearrange("(p t) j -> p t j", t=Q))
             av[half, h] = v
@@ -128,18 +129,24 @@ def tile_moe_bdx_mlp_silu_kernel(tc, dyT, a, w2, w1, gate, offs, pos1, pos2, out
 
         dneg = {}
 
-        def sig(half, h, pair):
-            z = pool.tile([P, Q, 256], F32, name="dneg", tag="dneg", bufs=6)
-            nc.scalar.activation(z[:], av[half, h][:, :, 256 * pair : 256 * (pair + 1)], SIGMOID)
-            dneg[half, h, pair] = z
+        def saved(e, h):
+            return av[e // 4, h][:, :, C * (e % 4) : C * (e % 4 + 1)]
 
-        def t1(half, h, pair):
-            z, v = dneg[half, h, pair], av[half, h][:, :, 256 * pair : 256 * (pair + 1)]
-            nc.vector.scalar_tensor_tensor(out=v, in0=z[:], scalar=1.0, in1=v, op0=SUB, op1=MULT)
+        def sig(e):
+            for h in range(2):
+                z = pool.tile([P, Q, C], F32, name="dneg", tag="dneg", bufs=4)
+                nc.scalar.activation(z[:], saved(e, h), SIGMOID)
+                dneg[e, h] = z
 
-        def zz(half, h, pair):
-            z, v = dneg[half, h, pair], av[half, h][:, :, 256 * pair : 256 * (pair + 1)]
-            nc.vector.scalar_tensor_tensor(out=z[:], in0=v, scalar=1.0, in1=z[:], op0=SUB, op1=MULT)
+        def t1(e):
+            for h in range(2):
+                v = saved(e, h)
+                nc.vector.scalar_tensor_tensor(out=v, in0=dneg[e, h][:], scalar=1.0, in1=v, op0=SUB, op1=MULT)
+
+        def zz(e):
+            for h in range(2):
+                z = dneg[e, h][:]
+                nc.vector.scalar_tensor_tensor(out=z, in0=saved(e, h), scalar=1.0, in1=z, op0=SUB, op1=MULT)
 
         wb, wcodes, wscales = {}, {}, {}
 
@@ -178,24 +185,23 @@ def tile_moe_bdx_mlp_silu_kernel(tc, dyT, a, w2, w1, gate, offs, pos1, pos2, out
 
         dh = {}
 
-        def mm1(e):
+        def mm1(e, h):
             half = e // 4
             slots = slice(C * (e % 4), C * (e % 4 + 1))
-            for h in range(2):
-                acc = psum.tile([P, Q, C], F32, name="dh", tag="dh", bufs=6)
-                for t in range(Q):
-                    cols = slice(P * t, P * (t + 1))
-                    for c in range(2):
-                        nc.tensor.matmul_mx(
-                            out=acc[:, t, :],
-                            lhsT=wcodes[e, c, h][:, cols].bitcast(FP8X4),
-                            lhsT_scale=wscales[e, c, h][:, cols],
-                            rhs=gcodes[c, half][:, slots].bitcast(FP8X4),
-                            rhs_scale=gscales[c, half][:, slots],
-                            start=(c == 0),
-                            stop=(c == 1),
-                        )
-                dh[e, h] = acc
+            acc = psum.tile([P, Q, C], F32, name="dh", tag="dh", bufs=6)
+            for t in range(Q):
+                cols = slice(P * t, P * (t + 1))
+                for c in range(2):
+                    nc.tensor.matmul_mx(
+                        out=acc[:, t, :],
+                        lhsT=wcodes[e, c, h][:, cols].bitcast(FP8X4),
+                        lhsT_scale=wscales[e, c, h][:, cols],
+                        rhs=gcodes[c, half][:, slots].bitcast(FP8X4),
+                        rhs_scale=gscales[c, half][:, slots],
+                        start=(c == 0),
+                        stop=(c == 1),
+                    )
+            dh[e, h] = acc
 
         dab, dacodes, dascales = {}, {}, {}
 
@@ -203,12 +209,11 @@ def tile_moe_bdx_mlp_silu_kernel(tc, dyT, a, w2, w1, gate, offs, pos1, pos2, out
             if h == 0:
                 b = pool.tile([P, 2, C, Q], BF16, name="dab", tag="dab", bufs=2, align_bytes=64)
                 dab[e] = b
-            slots = slice(C * (e % 2), C * (e % 2 + 1))
             nc.vector.scalar_tensor_tensor(
                 out=dab[e][:, h],
                 in0=dh[e, h][:].rearrange("p t j -> p j t"),
                 scalar=-1.0,
-                in1=dneg[e // 4, h, (e % 4) // 2][:, :, slots].rearrange("p t j -> p j t"),
+                in1=dneg[e, h][:].rearrange("p t j -> p j t"),
                 op0=MULT,
                 op1=MULT,
             )
@@ -226,11 +231,14 @@ def tile_moe_bdx_mlp_silu_kernel(tc, dyT, a, w2, w1, gate, offs, pos1, pos2, out
         dxp = {}
 
         def mm2(e):
-            acc = psum.tile([P, C], F32, name="dx", tag="dx", bufs=2)
+            if e % 4 == 0:
+                bank = psum.tile([P, HALF], F32, name="dx", tag="dx", bufs=2)
+                dxp[e // 4] = bank
+            acc = dxp[e // 4][:, C * (e % 4) : C * (e % 4 + 1)]
             for h in range(2):
                 x = 2 * (e % 2) + h
                 nc.tensor.matmul_mx(
-                    out=acc[:],
+                    out=acc,
                     lhsT=w1codes[e // 2][:, x, :].bitcast(FP8X4),
                     lhsT_scale=w1scales[e // 2][:, x, :],
                     rhs=dacodes[e][:, h, :].bitcast(FP8X4),
@@ -238,26 +246,27 @@ def tile_moe_bdx_mlp_silu_kernel(tc, dyT, a, w2, w1, gate, offs, pos1, pos2, out
                     start=(h == 0),
                     stop=(h == 1),
                 )
-            dxp[e] = acc
 
         def dxc(e):
-            nc.scalar.copy(out=dx_sb[:, C * e : C * (e + 1)], in_=dxp[e][:])
+            if e % 4 == 3:
+                half = e // 4
+                nc.scalar.copy(out=dx_sb[:, HALF * half : HALF * (half + 1)], in_=dxp[half][:])
 
         load_lists()
         load_gate(0)
         for t in range(Q):
             load_dy(0, t)
-            if t == 3:
+            if t == 2:
                 load_w2(0, 0, 0)
         load_dy(1, 0)
         load_dy(1, 1)
         load_w2(0, 0, 1)
         load_dy(1, 2)
         load_dy(1, 3)
-        load_a(0, 0)
         load_w2(0, 1, 0)
-        load_a(0, 1)
+        load_a(0, 0)
         load_w2(0, 1, 1)
+        load_a(0, 1)
         load_w1(0)
         load_gate(1)
         load_pos()
@@ -266,26 +275,25 @@ def tile_moe_bdx_mlp_silu_kernel(tc, dyT, a, w2, w1, gate, offs, pos1, pos2, out
                 load_w2(e, 0)
                 load_w2(e, 1)
             else:
-                load_w1(3)
                 for h in range(2):
                     for c in range(2):
                         load_w2(e, c, h)
-            if e in (2, 4):
-                load_w1(e // 2)
-            if e == 2:
+            if e in (2, 5, 7):
+                load_w1((2, 5, 7).index(e) + 1)
+            if e == 3:
                 load_a(1, 0)
                 load_a(1, 1)
 
         def background(item):
             op, args = item[0], [int(x) for x in item[1:]]
-            {"G": gather, "I": gint, "Q": qg, "S": sig, "T": t1, "Z": zz, "W": w1i, "R": w1q}[op](*args)
+            {"G": gather, "I": gint, "Q": qg, "W": w1i, "R": w1q}[op](*args)
 
         for t in range(Q):
             gather(0, 0, t)
         pieces = [(e, c, h) for e in range(E - 1) for c in range(2) for h in range(2)]
         pieces += [(E - 1, c, h) for h in range(2) for c in range(2)]
-        stages = {"mm1": mm1, "da0": lambda e: da(e, 0), "da1": lambda e: da(e, 1), "qda": qda, "mm2": mm2, "dxc": dxc}
-        for g in range(4 * E + 10):
+        stages = {"mm10": lambda e: mm1(e, 0), "mm11": lambda e: mm1(e, 1), "sig": sig, "t1": t1, "z": zz, "da0": lambda e: da(e, 0), "da1": lambda e: da(e, 1), "qda": qda, "mm2": mm2, "dxc": dxc}
+        for g in range(4 * E + 14):
             if g < 4 * E:
                 inter(*pieces[g])
             for at, item in BACKGROUND:
@@ -294,8 +302,11 @@ def tile_moe_bdx_mlp_silu_kernel(tc, dyT, a, w2, w1, gate, offs, pos1, pos2, out
             if 1 <= g <= 4 * E:
                 qw(*pieces[g - 1])
             for lag, stage in LAGS:
-                if g >= lag and (g - lag) % 4 == 0 and (g - lag) // 4 < E:
+                if g >= lag and (g - lag) % 4 == 0 and (g - lag) // 4 < E - 1:
                     stages[stage]((g - lag) // 4)
+            for lag, stage in LAST:
+                if g - lag == 4 * (E - 1):
+                    stages[stage](E - 1)
 
         for s in range(2):
             lst = slice(16 * s, 16 * (s + 1))

@@ -25,10 +25,10 @@ PAD = 8
 FLOPS = 2 * S * H * (N + K)
 BYTES = 4 * (N * T + H * S + E * N * H + E * H * K + S + K * T) + 2 * (128 * 64 + 2 * 128 * 32)
 
-VECTOR_PIECES = {(7, 1, 0), (7, 0, 0), (2, 0, 1), (4, 0, 0), (4, 1, 1), (2, 0, 0), (0, 1, 0), (5, 1, 0), (2, 1, 0)}
-BACKGROUND = [(0, "G100"), (0, "G102"), (2, "G103"), (2, "G010"), (2, "I00"), (3, "G013"), (4, "Q00"), (4, "G011"), (5, "G101"), (6, "W0"), (6, "I10"), (8, "G110"), (9, "Q10"), (11, "G111"), (12, "G112"), (12, "W1"), (12, "G012"), (12, "R0"), (13, "I01"), (14, "G113"), (17, "Q01"), (18, "I11"), (18, "W2"), (19, "R1"), (20, "Q11"), (20, "R2"), (25, "W3"), (34, "R3")]
-LAST = [(9, "qda"), (13, "mm2"), (5, "mm11"), (1, "sig"), (1, "t1"), (7, "da0"), (3, "mm10"), (7, "da1"), (13, "dxc"), (3, "z")]
-LAGS = [(10, "da0"), (13, "mm2"), (13, "dxc"), (1, "sig"), (10, "mm11"), (9, "mm10"), (3, "t1"), (4, "z"), (12, "qda"), (10, "da1")]
+VECTOR_PIECES = {(6, 1, 1), (5, 1, 1), (5, 0, 1), (7, 1, 1), (3, 0, 1), (2, 1, 1), (1, 1, 1)}
+BACKGROUND = [(0, "W0"), (0, "I00"), (0, "G100"), (0, "G101"), (0, "G102"), (1, "G103"), (1, "R0"), (2, "G010"), (2, "W1"), (2, "Q00"), (3, "W2"), (3, "I10"), (4, "G011"), (5, "G012"), (5, "Q10"), (5, "R1"), (8, "G013"), (10, "G110"), (10, "I01"), (11, "G111"), (12, "R2"), (14, "G112"), (15, "G113"), (16, "I11"), (18, "Q01"), (18, "W3"), (21, "Q11"), (34, "R3")]
+LAST = [(4, "sig"), (7, "da0"), (6, "mm11"), (7, "da1"), (7, "qda"), (13, "dxc"), (12, "mm2"), (5, "z"), (3, "mm10"), (4, "t1")]
+LAGS = [(3, "sig"), (5, "z"), (6, "mm11"), (10, "da1"), (5, "mm10"), (10, "qda"), (3, "t1"), (11, "mm2"), (9, "da0"), (11, "dxc")]
 
 
 def tile_moe_bdx_mlp_silu_kernel(tc, dyT, a, w2, w1, gate, offs, pos1, pos2, out):
@@ -253,36 +253,45 @@ def tile_moe_bdx_mlp_silu_kernel(tc, dyT, a, w2, w1, gate, offs, pos1, pos2, out
                 nc.scalar.copy(out=dx_sb[:, HALF * half : HALF * (half + 1)], in_=dxp[half][:])
 
         load_lists()
+        load_dy(0, 0)
         load_gate(0)
-        for t in range(Q):
-            load_dy(0, t)
-            if t == 2:
-                load_w2(0, 0, 0)
-        load_dy(1, 0)
-        load_dy(1, 1)
-        load_w2(0, 0, 1)
-        load_dy(1, 2)
-        load_dy(1, 3)
-        load_w2(0, 1, 0)
-        load_a(0, 0)
-        load_w2(0, 1, 1)
-        load_a(0, 1)
-        load_w1(0)
+        load_dy(0, 1)
         load_gate(1)
+        load_w2(0, 0, 0)
+        load_a(0, 0)
+        load_w2(0, 0, 1)
+        load_dy(0, 2)
+        load_w2(0, 1, 0)
+        load_w1(0)
+        load_w2(0, 1, 1)
+        load_dy(0, 3)
+        load_w2(1, 0)
+        load_w2(1, 1)
+        load_dy(1, 0)
+        load_a(0, 1)
+        load_dy(1, 1)
+        load_w2(2, 0)
+        load_dy(1, 2)
+        load_w2(2, 1)
+        load_w2(3, 0)
+        load_w2(3, 1)
+        load_w2(4, 0)
+        load_a(1, 0)
+        load_w2(4, 1)
+        load_dy(1, 3)
+        load_w1(1)
+        load_w1(2)
+        load_w2(5, 0)
+        load_w2(5, 1)
+        load_w2(6, 0)
+        load_w2(6, 1)
+        load_w1(3)
+        load_a(1, 1)
+        load_w2(7, 0, 0)
         load_pos()
-        for e in range(1, E):
-            if e < E - 1:
-                load_w2(e, 0)
-                load_w2(e, 1)
-            else:
-                for h in range(2):
-                    for c in range(2):
-                        load_w2(e, c, h)
-            if e in (2, 5, 7):
-                load_w1((2, 5, 7).index(e) + 1)
-            if e == 3:
-                load_a(1, 0)
-                load_a(1, 1)
+        load_w2(7, 1, 0)
+        load_w2(7, 0, 1)
+        load_w2(7, 1, 1)
 
         def background(item):
             op, args = item[0], [int(x) for x in item[1:]]

@@ -25,10 +25,10 @@ PAD = 8
 FLOPS = 2 * S * H * (N + K)
 BYTES = 4 * (N * T + H * S + E * N * H + E * H * K + S + K * T) + 2 * (128 * 64 + 2 * 128 * 32)
 
-VECTOR_PIECES = {(6, 1, 1), (5, 1, 1), (5, 0, 1), (7, 1, 1), (3, 0, 1), (2, 1, 1), (1, 1, 1)}
-BACKGROUND = [(0, "W0"), (0, "I00"), (0, "G100"), (0, "G101"), (0, "G102"), (1, "G103"), (1, "R0"), (2, "G010"), (2, "W1"), (2, "Q00"), (3, "W2"), (3, "I10"), (4, "G011"), (5, "G012"), (5, "Q10"), (5, "R1"), (8, "G013"), (10, "G110"), (10, "I01"), (11, "G111"), (12, "R2"), (14, "G112"), (15, "G113"), (16, "I11"), (18, "Q01"), (18, "W3"), (21, "Q11"), (34, "R3")]
-LAST = [(4, "sig"), (7, "da0"), (6, "mm11"), (7, "da1"), (7, "qda"), (13, "dxc"), (12, "mm2"), (5, "z"), (3, "mm10"), (4, "t1")]
-LAGS = [(3, "sig"), (5, "z"), (6, "mm11"), (10, "da1"), (5, "mm10"), (10, "qda"), (3, "t1"), (11, "mm2"), (9, "da0"), (11, "dxc")]
+VECTOR_PIECES = {(1, 1, 1), (6, 0, 1), (7, 0, 1), (2, 1, 1), (1, 0, 1), (3, 1, 1), (4, 0, 1), (4, 1, 1), (6, 1, 1), (5, 0, 1), (2, 0, 1)}
+BACKGROUND = [(0, "G100"), (0, "G101"), (0, "G102"), (0, "G103"), (0, "G010"), (0, "G011"), (0, "G012"), (0, "G013"), (0, "G110"), (0, "G111"), (0, "G112"), (0, "I00"), (0, "G113"), (2, "I10"), (2, "Q00"), (2, "W0"), (2, "I01"), (3, "Q10"), (4, "R0"), (5, "W1"), (7, "Q01"), (10, "I11"), (12, "W2"), (13, "Q11"), (17, "R1"), (18, "R2"), (32, "W3"), (34, "R3")]
+LAST = [(9, "qda"), (5, "t1"), (10, "mm2"), (13, "dxc"), (4, "mm10"), (5, "z"), (6, "da1"), (5, "da0"), (4, "mm11"), (4, "sig")]
+LAGS = [(13, "dxc"), (2, "t1"), (1, "sig"), (12, "mm2"), (11, "qda"), (9, "da0"), (6, "mm11"), (9, "da1"), (4, "mm10"), (2, "z")]
 
 
 def tile_moe_bdx_mlp_silu_kernel(tc, dyT, a, w2, w1, gate, offs, pos1, pos2, out):
@@ -134,7 +134,7 @@ def tile_moe_bdx_mlp_silu_kernel(tc, dyT, a, w2, w1, gate, offs, pos1, pos2, out
 
         def sig(e):
             for h in range(2):
-                z = pool.tile([P, Q, C], F32, name="dneg", tag="dneg", bufs=4)
+                z = pool.tile([P, Q, C], F32, name="dneg", tag="dy", bufs=8)
                 nc.scalar.activation(z[:], saved(e, h), SIGMOID)
                 dneg[e, h] = z
 
@@ -151,7 +151,7 @@ def tile_moe_bdx_mlp_silu_kernel(tc, dyT, a, w2, w1, gate, offs, pos1, pos2, out
         wb, wcodes, wscales = {}, {}, {}
 
         def inter(e, c, h):
-            b = pool.tile([P, 512 * Q], BF16, name="wb", tag="wb", bufs=5, align_bytes=64)
+            b = pool.tile([P, 512 * Q], BF16, name="wb", tag="wb", bufs=7, align_bytes=64)
             dst = b[:].rearrange("p (t m j) -> p m j t", t=4, j=Q)
             src = raw[e, c, h].rearrange("p j (m t) -> p m j t", t=4)
             if (e, c, h) in VECTOR_PIECES:
@@ -253,42 +253,42 @@ def tile_moe_bdx_mlp_silu_kernel(tc, dyT, a, w2, w1, gate, offs, pos1, pos2, out
                 nc.scalar.copy(out=dx_sb[:, HALF * half : HALF * (half + 1)], in_=dxp[half][:])
 
         load_lists()
+        load_w2(0, 0, 0)
+        load_w2(0, 0, 1)
         load_dy(0, 0)
         load_gate(0)
         load_dy(0, 1)
-        load_gate(1)
-        load_w2(0, 0, 0)
-        load_a(0, 0)
-        load_w2(0, 0, 1)
         load_dy(0, 2)
         load_w2(0, 1, 0)
-        load_w1(0)
-        load_w2(0, 1, 1)
         load_dy(0, 3)
+        load_dy(1, 0)
+        load_a(0, 0)
+        load_dy(1, 1)
+        load_w2(0, 1, 1)
+        load_dy(1, 2)
+        load_dy(1, 3)
+        load_w1(0)
+        load_gate(1)
         load_w2(1, 0)
         load_w2(1, 1)
-        load_dy(1, 0)
-        load_a(0, 1)
-        load_dy(1, 1)
         load_w2(2, 0)
-        load_dy(1, 2)
         load_w2(2, 1)
         load_w2(3, 0)
         load_w2(3, 1)
-        load_w2(4, 0)
-        load_a(1, 0)
-        load_w2(4, 1)
-        load_dy(1, 3)
         load_w1(1)
-        load_w1(2)
+        load_w2(4, 0)
+        load_w2(4, 1)
         load_w2(5, 0)
         load_w2(5, 1)
         load_w2(6, 0)
         load_w2(6, 1)
-        load_w1(3)
-        load_a(1, 1)
-        load_w2(7, 0, 0)
+        load_a(0, 1)
         load_pos()
+        load_a(1, 0)
+        load_w2(7, 0, 0)
+        load_a(1, 1)
+        load_w1(2)
+        load_w1(3)
         load_w2(7, 1, 0)
         load_w2(7, 0, 1)
         load_w2(7, 1, 1)

@@ -25,10 +25,10 @@ PAD = 8
 FLOPS = 2 * S * H * (N + K)
 BYTES = 4 * (N * T + H * S + E * N * H + E * H * K + S + K * T) + 2 * (128 * 64 + 2 * 128 * 32)
 
-VECTOR_PIECES = {(1, 1, 1), (6, 0, 1), (7, 0, 1), (2, 1, 1), (1, 0, 1), (3, 1, 1), (4, 0, 1), (4, 1, 1), (6, 1, 1), (5, 0, 1), (2, 0, 1)}
-BACKGROUND = [(0, "G100"), (0, "G101"), (0, "G102"), (0, "G103"), (0, "G010"), (0, "G011"), (0, "G012"), (0, "G013"), (0, "G110"), (0, "G111"), (0, "G112"), (0, "I00"), (0, "G113"), (2, "I10"), (2, "Q00"), (2, "W0"), (2, "I01"), (3, "Q10"), (4, "R0"), (5, "W1"), (7, "Q01"), (10, "I11"), (12, "W2"), (13, "Q11"), (17, "R1"), (18, "R2"), (32, "W3"), (34, "R3")]
-LAST = [(9, "qda"), (5, "t1"), (10, "mm2"), (13, "dxc"), (4, "mm10"), (5, "z"), (6, "da1"), (5, "da0"), (4, "mm11"), (4, "sig")]
-LAGS = [(13, "dxc"), (2, "t1"), (1, "sig"), (12, "mm2"), (11, "qda"), (9, "da0"), (6, "mm11"), (9, "da1"), (4, "mm10"), (2, "z")]
+VECTOR_PIECES = {(2, 1, 1), (6, 0, 1), (1, 1, 1), (5, 0, 1), (2, 0, 1), (4, 0, 1), (6, 1, 1)}
+BACKGROUND = [(0, "I00"), (0, "G100"), (0, "W0"), (0, "Q00"), (0, "G101"), (1, "G102"), (2, "G103"), (3, "I10"), (4, "Q10"), (4, "R0"), (5, "W1"), (6, "G010"), (8, "G011"), (9, "G012"), (9, "G013"), (9, "G110"), (10, "W2"), (10, "G111"), (11, "I01"), (12, "R1"), (14, "G112"), (14, "Q01"), (15, "R2"), (15, "G113"), (18, "I11"), (21, "Q11"), (24, "W3"), (27, "R3")]
+LAST = [(3, "t1"), (3, "mm10"), (1, "sig"), (12, "dxc"), (3, "z"), (4, "da0"), (5, "mm11"), (9, "qda"), (11, "mm2"), (5, "da1")]
+LAGS = [(7, "da1"), (2, "t1"), (13, "dxc"), (6, "mm10"), (4, "z"), (12, "mm2"), (1, "sig"), (11, "qda"), (5, "mm11"), (6, "da0")]
 
 
 def tile_moe_bdx_mlp_silu_kernel(tc, dyT, a, w2, w1, gate, offs, pos1, pos2, out):
@@ -127,7 +127,7 @@ def tile_moe_bdx_mlp_silu_kernel(tc, dyT, a, w2, w1, gate, offs, pos1, pos2, out
             )
             gcodes[c, half], gscales[c, half] = codes, scales
 
-        dneg = {}
+        dneg, ut = {}, {}
 
         def saved(e, h):
             return av[e // 4, h][:, :, C * (e % 4) : C * (e % 4 + 1)]
@@ -140,13 +140,16 @@ def tile_moe_bdx_mlp_silu_kernel(tc, dyT, a, w2, w1, gate, offs, pos1, pos2, out
 
         def t1(e):
             for h in range(2):
-                v = saved(e, h)
-                nc.vector.scalar_tensor_tensor(out=v, in0=dneg[e, h][:], scalar=1.0, in1=v, op0=SUB, op1=MULT)
+                u = pool.tile([P, Q, C], F32, name="u", tag="u", bufs=2)
+                nc.vector.scalar_tensor_tensor(
+                    out=u[:], in0=dneg[e, h][:], scalar=1.0, in1=saved(e, h), op0=SUB, op1=MULT
+                )
+                ut[e, h] = u
 
         def zz(e):
             for h in range(2):
                 z = dneg[e, h][:]
-                nc.vector.scalar_tensor_tensor(out=z, in0=saved(e, h), scalar=1.0, in1=z, op0=SUB, op1=MULT)
+                nc.vector.scalar_tensor_tensor(out=z, in0=ut[e, h][:], scalar=1.0, in1=z, op0=SUB, op1=MULT)
 
         wb, wcodes, wscales = {}, {}, {}
 
@@ -253,45 +256,45 @@ def tile_moe_bdx_mlp_silu_kernel(tc, dyT, a, w2, w1, gate, offs, pos1, pos2, out
                 nc.scalar.copy(out=dx_sb[:, HALF * half : HALF * (half + 1)], in_=dxp[half][:])
 
         load_lists()
-        load_w2(0, 0, 0)
-        load_w2(0, 0, 1)
         load_dy(0, 0)
         load_gate(0)
         load_dy(0, 1)
         load_dy(0, 2)
+        load_w2(0, 0, 0)
+        load_gate(1)
+        load_w2(0, 0, 1)
         load_w2(0, 1, 0)
         load_dy(0, 3)
         load_dy(1, 0)
-        load_a(0, 0)
         load_dy(1, 1)
         load_w2(0, 1, 1)
         load_dy(1, 2)
-        load_dy(1, 3)
-        load_w1(0)
-        load_gate(1)
         load_w2(1, 0)
+        load_w1(0)
+        load_a(0, 0)
+        load_dy(1, 3)
         load_w2(1, 1)
         load_w2(2, 0)
         load_w2(2, 1)
         load_w2(3, 0)
+        load_a(0, 1)
         load_w2(3, 1)
-        load_w1(1)
         load_w2(4, 0)
+        load_w1(1)
         load_w2(4, 1)
         load_w2(5, 0)
-        load_w2(5, 1)
-        load_w2(6, 0)
-        load_w2(6, 1)
-        load_a(0, 1)
         load_pos()
         load_a(1, 0)
-        load_w2(7, 0, 0)
+        load_w2(5, 1)
+        load_w2(6, 0)
         load_a(1, 1)
+        load_w2(6, 1)
         load_w1(2)
-        load_w1(3)
+        load_w2(7, 0, 0)
         load_w2(7, 1, 0)
         load_w2(7, 0, 1)
         load_w2(7, 1, 1)
+        load_w1(3)
 
         def background(item):
             op, args = item[0], [int(x) for x in item[1:]]

from contextlib import ExitStack

import concourse.mybir as mybir

F32 = mybir.dt.float32
BF16 = mybir.dt.bfloat16
U32 = mybir.dt.uint32
U16 = mybir.dt.uint16
U8 = mybir.dt.uint8
FP8X4 = mybir.dt.float8_e4m3fn_x4

MULT = mybir.AluOpType.mult
ADD = mybir.AluOpType.add
SUB = mybir.AluOpType.subtract
SIGMOID = mybir.ActivationFunctionType.Sigmoid

P = 128
E, C, T = 8, 128, 512
N, H, K = 1024, 1024, 128
S = E * C
Q = 4
HALF = S // 2
PAD = 8

FLOPS = 2 * S * H * (N + K)
BYTES = 4 * (N * T + H * S + E * N * H + E * H * K + S + K * T) + 2 * (128 * 64 + 2 * 128 * 32)

VECTOR_PIECES = {(2, 1, 1), (6, 0, 1), (1, 1, 1), (5, 0, 1), (2, 0, 1), (4, 0, 1), (6, 1, 1)}
BACKGROUND = [(0, "I00"), (0, "G100"), (0, "W0"), (0, "Q00"), (0, "G101"), (1, "G102"), (2, "G103"), (3, "I10"), (4, "Q10"), (4, "R0"), (5, "W1"), (6, "G010"), (8, "G011"), (9, "G012"), (9, "G013"), (9, "G110"), (10, "W2"), (10, "G111"), (11, "I01"), (12, "R1"), (14, "G112"), (14, "Q01"), (15, "R2"), (15, "G113"), (18, "I11"), (21, "Q11"), (24, "W3"), (27, "R3")]
LAST = [(3, "t1"), (3, "mm10"), (1, "sig"), (12, "dxc"), (3, "z"), (4, "da0"), (5, "mm11"), (9, "qda"), (11, "mm2"), (5, "da1")]
LAGS = [(7, "da1"), (2, "t1"), (13, "dxc"), (6, "mm10"), (4, "z"), (12, "mm2"), (1, "sig"), (11, "qda"), (5, "mm11"), (6, "da0")]


def tile_moe_bdx_mlp_silu_kernel(tc, dyT, a, w2, w1, gate, offs, pos1, pos2, out):
    nc = tc.nc
    with ExitStack() as ctx:
        pool = ctx.enter_context(tc.tile_pool(name="sb", bufs=1))
        psum = ctx.enter_context(tc.psum_pool(name="ps", bufs=1))

        warm = pool.tile([P, 8], F32, name="warm")
        nc.gpsimd.memset(warm[:], 0.0)
        nc.scalar.activation(warm[:], warm[:], SIGMOID)

        offs_sb = pool.tile([P, S // 16], U16, name="offs_sb")
        pos1_sb = pool.tile([P, T // 16], U16, name="pos1_sb")
        pos2_sb = pool.tile([P, T // 16], U16, name="pos2_sb")
        gate_sb = pool.tile([P, S], F32, name="gate_sb")
        dx_sb = pool.tile([P, S], F32, name="dx_sb")

        dy = {}
        for c in range(2):
            for t in range(Q):
                d = pool.tile([P, T + PAD], F32, name="dy", tag="dy", bufs=8)
                nc.gpsimd.memset(d[:, T:], 0.0)
                dy[c, t] = d

        def load_lists():
            nc.sync.dma_start(out=offs_sb[:], in_=offs)

        def load_pos():
            nc.sync.dma_start(out=pos1_sb[:], in_=pos1)
            nc.sync.dma_start(out=pos2_sb[:], in_=pos2)

        def load_dy(c, t):
            rows = dyT[512 * c : 512 * (c + 1), :].rearrange("(p t) j -> t p j", t=Q)
            nc.sync.dma_start(out=dy[c, t][:, 0:T], in_=rows[t, :, :])

        def load_gate(half):
            cols = slice(HALF * half, HALF * (half + 1))
            nc.sync.dma_start(out=gate_sb[:, cols], in_=gate[0:P, cols])

        raw = {}

        def load_w2(e, c, h=None):
            rows = w2[e, 512 * c : 512 * (c + 1), :].rearrange("(p j) i -> p j i", j=Q)
            if h is None:
                r = pool.tile([P, Q, H], F32, name="raw", tag="raw", bufs=4)
                nc.sync.dma_start(out=r[:], in_=rows)
                raw[e, c, 0] = r[:, :, 0:512]
                raw[e, c, 1] = r[:, :, 512:1024]
            else:
                r = pool.tile([P, Q, 512], F32, name="raw", tag="raw", bufs=4)
                nc.sync.dma_start(out=r[:], in_=rows[:, :, 512 * h : 512 * (h + 1)])
                raw[e, c, h] = r[:]

        av = {}

        def load_a(half, h):
            v = pool.tile([P, Q, HALF], F32, name="av", tag="av", bufs=4)
            cols = slice(HALF * half, HALF * (half + 1))
            nc.sync.dma_start(out=v[:], in_=a[512 * h : 512 * (h + 1), cols].rearrange("(p t) j -> p t j", t=Q))
            av[half, h] = v

        w1raw = {}

        def load_w1(pair):
            r = pool.tile([P, 4, Q, K], F32, name="w1raw", tag="w1raw", bufs=1)
            rows = w1[2 * pair : 2 * pair + 2, :, :].rearrange("e (h p j) k -> p (e h) j k", h=2, j=Q)
            nc.sync.dma_start(out=r[:], in_=rows)
            w1raw[pair] = r

        gf, gb, gcodes, gscales = {}, {}, {}, {}

        def gather(c, half, t):
            if t == 0:
                f = pool.tile([P, Q, HALF], F32, name="gf", tag="gf", bufs=2)
                gf[c, half] = f
            cols = slice(HALF * half, HALF * (half + 1))
            lst = slice(32 * half, 32 * (half + 1))
            nc.vector.tensor_tensor(
                gf[c, half][:, t, :], dy[c, t][:].indirect(offs_sb[:, lst]), gate_sb[:, cols], MULT
            )

        def gint(c, half):
            b = pool.tile([P, HALF, Q], BF16, name="gb", tag="gb", bufs=2, align_bytes=64)
            nc.scalar.copy(
                out=b[:].rearrange("p (c i) t -> p c t i", i=4),
                in_=gf[c, half][:].rearrange("p t (c i) -> p c t i", i=4),
            )
            gb[c, half] = b

        def qg(c, half):
            codes = pool.tile([P, HALF], U32, name="gcodes", tag="gcodes", bufs=4, align_bytes=64)
            scales = pool.tile([P, HALF], U8, name="gscales", tag="gscales", bufs=4, align_bytes=64)
            nc.vector.quantize_mx(
                out=codes[:].bitcast(FP8X4), scales=scales[:], in_=gb[c, half][:].rearrange("p s t -> p (s t)")
            )
            gcodes[c, half], gscales[c, half] = codes, scales

        dneg, ut = {}, {}

        def saved(e, h):
            return av[e // 4, h][:, :, C * (e % 4) : C * (e % 4 + 1)]

        def sig(e):
            for h in range(2):
                z = pool.tile([P, Q, C], F32, name="dneg", tag="dy", bufs=8)
                nc.scalar.activation(z[:], saved(e, h), SIGMOID)
                dneg[e, h] = z

        def t1(e):
            for h in range(2):
                u = pool.tile([P, Q, C], F32, name="u", tag="u", bufs=2)
                nc.vector.scalar_tensor_tensor(
                    out=u[:], in0=dneg[e, h][:], scalar=1.0, in1=saved(e, h), op0=SUB, op1=MULT
                )
                ut[e, h] = u

        def zz(e):
            for h in range(2):
                z = dneg[e, h][:]
                nc.vector.scalar_tensor_tensor(out=z, in0=ut[e, h][:], scalar=1.0, in1=z, op0=SUB, op1=MULT)

        wb, wcodes, wscales = {}, {}, {}

        def inter(e, c, h):
            b = pool.tile([P, 512 * Q], BF16, name="wb", tag="wb", bufs=7, align_bytes=64)
            dst = b[:].rearrange("p (t m j) -> p m j t", t=4, j=Q)
            src = raw[e, c, h].rearrange("p j (m t) -> p m j t", t=4)
            if (e, c, h) in VECTOR_PIECES:
                nc.vector.tensor_copy(out=dst, in_=src)
            else:
                nc.scalar.copy(out=dst, in_=src)
            wb[e, c, h] = b

        def qw(e, c, h):
            codes = pool.tile([P, 512], U32, name="wcodes", tag="wcodes", bufs=8, align_bytes=64)
            scales = pool.tile([P, 512], U8, name="wscales", tag="wscales", bufs=8, align_bytes=64)
            nc.vector.quantize_mx(out=codes[:].bitcast(FP8X4), scales=scales[:], in_=wb[e, c, h][:])
            wcodes[e, c, h], wscales[e, c, h] = codes, scales

        w1b, w1codes, w1scales = {}, {}, {}

        def w1i(pair):
            b = pool.tile([P, 4, K, Q], BF16, name="w1b", tag="w1b", bufs=1, align_bytes=64)
            nc.scalar.copy(out=b[:], in_=w1raw[pair][:].rearrange("p x j k -> p x k j"))
            w1b[pair] = b

        def w1q(pair):
            codes = pool.tile([P, 4, K], U32, name="w1codes", tag="w1codes", bufs=2, align_bytes=64)
            scales = pool.tile([P, 4, K], U8, name="w1scales", tag="w1scales", bufs=2, align_bytes=64)
            nc.vector.quantize_mx(
                out=codes[:].rearrange("p x k -> p (x k)").bitcast(FP8X4),
                scales=scales[:].rearrange("p x k -> p (x k)"),
                in_=w1b[pair][:].rearrange("p x k j -> p (x k j)"),
            )
            w1codes[pair], w1scales[pair] = codes, scales

        dh = {}

        def mm1(e, h):
            half = e // 4
            slots = slice(C * (e % 4), C * (e % 4 + 1))
            acc = psum.tile([P, Q, C], F32, name="dh", tag="dh", bufs=6)
            for t in range(Q):
                cols = slice(P * t, P * (t + 1))
                for c in range(2):
                    nc.tensor.matmul_mx(
                        out=acc[:, t, :],
                        lhsT=wcodes[e, c, h][:, cols].bitcast(FP8X4),
                        lhsT_scale=wscales[e, c, h][:, cols],
                        rhs=gcodes[c, half][:, slots].bitcast(FP8X4),
                        rhs_scale=gscales[c, half][:, slots],
                        start=(c == 0),
                        stop=(c == 1),
                    )
            dh[e, h] = acc

        dab, dacodes, dascales = {}, {}, {}

        def da(e, h):
            if h == 0:
                b = pool.tile([P, 2, C, Q], BF16, name="dab", tag="dab", bufs=2, align_bytes=64)
                dab[e] = b
            nc.vector.scalar_tensor_tensor(
                out=dab[e][:, h],
                in0=dh[e, h][:].rearrange("p t j -> p j t"),
                scalar=-1.0,
                in1=dneg[e, h][:].rearrange("p t j -> p j t"),
                op0=MULT,
                op1=MULT,
            )

        def qda(e):
            codes = pool.tile([P, 2, C], U32, name="dacodes", tag="dacodes", bufs=2, align_bytes=64)
            scales = pool.tile([P, 2, C], U8, name="dascales", tag="dascales", bufs=2, align_bytes=64)
            nc.vector.quantize_mx(
                out=codes[:].rearrange("p h j -> p (h j)").bitcast(FP8X4),
                scales=scales[:].rearrange("p h j -> p (h j)"),
                in_=dab[e][:].rearrange("p h j t -> p (h j t)"),
            )
            dacodes[e], dascales[e] = codes, scales

        dxp = {}

        def mm2(e):
            if e % 4 == 0:
                bank = psum.tile([P, HALF], F32, name="dx", tag="dx", bufs=2)
                dxp[e // 4] = bank
            acc = dxp[e // 4][:, C * (e % 4) : C * (e % 4 + 1)]
            for h in range(2):
                x = 2 * (e % 2) + h
                nc.tensor.matmul_mx(
                    out=acc,
                    lhsT=w1codes[e // 2][:, x, :].bitcast(FP8X4),
                    lhsT_scale=w1scales[e // 2][:, x, :],
                    rhs=dacodes[e][:, h, :].bitcast(FP8X4),
                    rhs_scale=dascales[e][:, h, :],
                    start=(h == 0),
                    stop=(h == 1),
                )

        def dxc(e):
            if e % 4 == 3:
                half = e // 4
                nc.scalar.copy(out=dx_sb[:, HALF * half : HALF * (half + 1)], in_=dxp[half][:])

        load_lists()
        load_dy(0, 0)
        load_gate(0)
        load_dy(0, 1)
        load_dy(0, 2)
        load_w2(0, 0, 0)
        load_gate(1)
        load_w2(0, 0, 1)
        load_w2(0, 1, 0)
        load_dy(0, 3)
        load_dy(1, 0)
        load_dy(1, 1)
        load_w2(0, 1, 1)
        load_dy(1, 2)
        load_w2(1, 0)
        load_w1(0)
        load_a(0, 0)
        load_dy(1, 3)
        load_w2(1, 1)
        load_w2(2, 0)
        load_w2(2, 1)
        load_w2(3, 0)
        load_a(0, 1)
        load_w2(3, 1)
        load_w2(4, 0)
        load_w1(1)
        load_w2(4, 1)
        load_w2(5, 0)
        load_pos()
        load_a(1, 0)
        load_w2(5, 1)
        load_w2(6, 0)
        load_a(1, 1)
        load_w2(6, 1)
        load_w1(2)
        load_w2(7, 0, 0)
        load_w2(7, 1, 0)
        load_w2(7, 0, 1)
        load_w2(7, 1, 1)
        load_w1(3)

        def background(item):
            op, args = item[0], [int(x) for x in item[1:]]
            {"G": gather, "I": gint, "Q": qg, "W": w1i, "R": w1q}[op](*args)

        for t in range(Q):
            gather(0, 0, t)
        pieces = [(e, c, h) for e in range(E - 1) for c in range(2) for h in range(2)]
        pieces += [(E - 1, c, h) for h in range(2) for c in range(2)]
        stages = {"mm10": lambda e: mm1(e, 0), "mm11": lambda e: mm1(e, 1), "sig": sig, "t1": t1, "z": zz, "da0": lambda e: da(e, 0), "da1": lambda e: da(e, 1), "qda": qda, "mm2": mm2, "dxc": dxc}
        for g in range(4 * E + 14):
            if g < 4 * E:
                inter(*pieces[g])
            for at, item in BACKGROUND:
                if at == g:
                    background(item)
            if 1 <= g <= 4 * E:
                qw(*pieces[g - 1])
            for lag, stage in LAGS:
                if g >= lag and (g - lag) % 4 == 0 and (g - lag) // 4 < E - 1:
                    stages[stage]((g - lag) // 4)
            for lag, stage in LAST:
                if g - lag == 4 * (E - 1):
                    stages[stage](E - 1)

        for s in range(2):
            lst = slice(16 * s, 16 * (s + 1))
            g1 = pool.tile([P, T // 2], F32, name="g1", tag="g1", bufs=2)
            g2 = pool.tile([P, T // 2], F32, name="g2", tag="g2", bufs=2)
            res = pool.tile([P, T // 2], F32, name="res", tag="res", bufs=2)
            nc.vector.tensor_copy(g1[:], dx_sb[:].indirect(pos1_sb[:, lst]))
            nc.vector.tensor_copy(g2[:], dx_sb[:].indirect(pos2_sb[:, lst]))
            nc.vector.tensor_tensor(res[:], g1[:], g2[:], ADD)
            nc.sync.dma_start(out=out[:, 256 * s : 256 * (s + 1)], in_=res[:])
